import numpy as np
import ml_dtypes


def mxq(x, axis, fmt="e4m3"):
    dtype, down = {"e4m3": (ml_dtypes.float8_e4m3fn, 7), "e5m2": (ml_dtypes.float8_e5m2, 14)}[fmt]
    v = np.moveaxis(np.asarray(x, np.float32).astype(ml_dtypes.bfloat16).astype(np.float64), axis, -1)
    blocks = v.reshape(v.shape[:-1] + (-1, 32))
    amax = np.abs(blocks).max(-1, keepdims=True)
    byte = np.maximum(np.where(amax > 0, np.frexp(amax)[1] - 1 + 127, 0) - down, 1)
    scale = np.exp2(byte - 127.0)
    codes = (blocks / scale).astype(np.float32).astype(dtype).astype(np.float64)
    return np.moveaxis((codes * scale).reshape(v.shape), -1, axis)


WIDE = False


def mx_kscale(k):
    if not WIDE:
        return np.ones(k)
    levels = np.array([24, -24, 12, -12, 0])
    if k % 512:
        return np.exp2(np.random.permutation(np.resize(levels, k // 32))).repeat(32)
    a = np.empty((k // 512, 16))
    for p in range(k // 512):
        a[p, :8] = np.random.permutation(np.resize(levels, 8))
        for g in range(8):
            far = levels[np.abs(levels - a[p, g]) >= 10]
            a[p, g + 8] = far[np.random.randint(len(far))]
    return np.exp2(a.ravel()).repeat(32)


def f64(x):
    return np.asarray(x).astype(np.float64)


def striped8(idx):
    return np.concatenate([v.reshape(-1, 16).T for v in idx]).astype(np.uint16)


def unstriped8(offs):
    return np.stack([offs[16 * g:16 * g + 16].T.reshape(-1) for g in range(8)]).astype(np.int64)


E2M1 = np.array([0.0, 0.5, 1.0, 1.5, 2.0, 3.0, 4.0, 6.0, -0.0, -0.5, -1.0, -1.5, -2.0, -3.0, -4.0, -6.0])


def pack_weight(w, fmt):
    k, n = w.shape
    w = f64(np.asarray(w, np.float32).astype(ml_dtypes.bfloat16)).reshape(k // 32, 32, n)
    amax = np.abs(w).max(1)
    if fmt == "e4m3":
        byte = np.frexp(amax)[1] - 1 + 127 - 7
    else:
        mant, ex = np.frexp(amax / 6.0)
        byte = np.where(mant > 0.5, ex, ex - 1) + 127
    byte = np.clip(np.where(amax > 0, byte, 1), 1, 254)
    scaled = (w * np.exp2(127.0 - byte)[:, None, :]).reshape(k, n).astype(np.float32)
    by_word = np.ascontiguousarray(scaled.reshape(k // 512, 128, 4, n).transpose(0, 1, 3, 2))
    if fmt == "e4m3":
        words = by_word.astype(ml_dtypes.float8_e4m3fn).view(np.uint8)
    else:
        c = by_word.astype(ml_dtypes.float4_e2m1fn).view(np.uint8) & 0xF
        words = (c[..., 0::2] | (c[..., 1::2] << 4)).reshape(k // 512, 128, 2 * n)
    return np.ascontiguousarray(words), np.ascontiguousarray(byte.astype(np.uint8).reshape(k // 512, 16, n))


def unpack_weight(words, scales, fmt):
    g, _, n = scales.shape
    words = np.ascontiguousarray(words).reshape(g, 128, n, -1)
    if fmt == "e4m3":
        vals = words.view(ml_dtypes.float8_e4m3fn).astype(np.float64)
    else:
        nib = np.empty((g, 128, n, 4), np.uint8)
        nib[..., 0::2] = words & 0xF
        nib[..., 1::2] = words >> 4
        vals = E2M1[nib]
    vals = vals * np.repeat(np.exp2(scales.astype(np.float64) - 127.0), 8, axis=1)[..., None]
    return vals.transpose(0, 1, 3, 2).reshape(g * 512, n)


def planes(y):
    n, m = y.shape
    v = y.astype(np.float32).astype(ml_dtypes.bfloat16).astype(np.float64).reshape(n // 32, 32, m)
    top = np.abs(v).max(1)
    byte = np.clip(np.where(top > 0, np.frexp(top)[1] - 1 + 127 - 7, 1), 1, 254)
    codes = (v * np.exp2(127.0 - byte)[:, None, :]).reshape(n, m).astype(np.float32).astype(ml_dtypes.float8_e4m3fn).view(np.uint8)
    words = codes.reshape(n // 512, 128, 4, m).transpose(0, 1, 3, 2)
    return np.ascontiguousarray(words), np.ascontiguousarray(byte.astype(np.uint8).reshape(n // 512, 16, m))


def sigm(f):
    return 1.0 / (1.0 + np.exp(-np.maximum(f, -700.0)))


K, L, N, T, J = 512, 512, 512, 2048, 1024


def setup_inputs():
    n = np.random.standard_normal
    s = mx_kscale(K)[:, None]
    s2 = mx_kscale(L)[:, None]
    p_wa = pack_weight(n((K, N)) / np.sqrt(K) / s, "e2m1")
    return {
        "xT": (n((K, T)) * s).astype(np.float32),
        "wgt": np.repeat(np.random.uniform(0.5, 2.0, (8, J)), 16, axis=0).astype(np.float32),
        "zT": (n((L, T)) * s2).astype(np.float32),
        "wgt2": np.repeat(np.random.uniform(0.5, 2.0, (8, J)), 16, axis=0).astype(np.float32),
        "wa_words": p_wa[0],
        "wa_scales": p_wa[1],
        "wb": (n((L, N)) / np.sqrt(L) / s2).astype(np.float32),
        "res": (n((N, J))).astype(np.float32),
        "offs": striped8(np.stack([np.random.permutation(T)[:J] for _ in range(8)])),
        "offs2": striped8(np.stack([np.random.permutation(T)[:J] for _ in range(8)])),
    }


def reference(xT, wgt, zT, wgt2, wa_words, wa_scales, wb, res, offs, offs2):
    idx = unstriped8(offs)
    idx2 = unstriped8(offs2)
    rows = np.arange(K)
    xg = f64(wgt)[rows // 4 % 128] * f64(xT)[rows[:, None], idx[rows % 512 // 64]]
    xT_ = mxq(xg, 0, "e4m3")
    rows = np.arange(L)
    xg = f64(wgt2)[rows // 4 % 128] * f64(zT)[rows[:, None], idx2[rows % 512 // 64]]
    zT_ = mxq(xg, 0, "e4m3")
    wa_ = unpack_weight(wa_words, wa_scales, "e2m1")
    wb_ = mxq(f64(wb), 0, "e4m3")
    ya = wa_.T @ xT_
    yb = wb_.T @ zT_
    out_0 = ya * sigm(yb) + f64(res)
    return (out_0,) + planes(out_0)

@@ -1,0 +1,209 @@
+from contextlib import ExitStack
+
+import concourse.mybir as mybir
+
+K, N, T, J = 512, 512, 2048, 1024
+FLOPS = 2 * 2 * K * N * J
+
+F32 = mybir.dt.float32
+BF16 = mybir.dt.bfloat16
+I32 = mybir.dt.int32
+U32 = mybir.dt.uint32
+U16 = mybir.dt.uint16
+U8 = mybir.dt.uint8
+E4M3 = mybir.dt.float8_e4m3fn_x4
+E2M1 = mybir.dt.float4_e2m1fn_x4
+MULT = mybir.AluOpType.mult
+ADD = mybir.AluOpType.add
+SIGMOID = mybir.ActivationFunctionType.Sigmoid
+
+P = 128
+PACK = 4
+CHUNK = 256
+CHUNKS = J // CHUNK
+HALF = J // 2
+
+
+def interleave(engine_copy, dst, src):
+    engine_copy(out=dst.rearrange("p (c i) t -> p c t i", i=4), in_=src.rearrange("p t (c i) -> p c t i", i=4))
+
+
+def tile_list_gate_resP_kernel(
+    tc, xT, wgt, zT, wgt2, wa_words, wa_scales, wb, res, offs, offs2, out_0, out_1, out_2
+):
+    nc = tc.nc
+    with ExitStack() as ctx:
+        keep = ctx.enter_context(tc.tile_pool(name="keep", bufs=1))
+        ring = ctx.enter_context(tc.tile_pool(name="ring", bufs=2))
+        psum = ctx.enter_context(tc.psum_pool(name="psum", bufs=8))
+
+        x_list = keep.tile([P, J // 16], U16, name="x_list")
+        z_list = keep.tile([P, J // 16], U16, name="z_list")
+        x_planes = [keep.tile([P, T], F32, name=f"x_plane{t}") for t in range(PACK)]
+        z_planes = [keep.tile([P, T], F32, name=f"z_plane{t}") for t in range(PACK)]
+        x_wgt = keep.tile([P, J], F32, name="x_wgt")
+        z_wgt = keep.tile([P, J], F32, name="z_wgt")
+        wa_raw = keep.tile([P, 2 * N], U8, name="wa_raw", align_bytes=64)
+        wa_sraw = keep.tile([P, N], U8, name="wa_sraw", align_bytes=64)
+        wa_codes = keep.tile([P, 2 * N], U8, name="wa_codes", align_bytes=64)
+        wa_sc = keep.tile([P, N], U8, name="wa_sc", align_bytes=64)
+        wb_raw = keep.tile([P, PACK, N], F32, name="wb_raw")
+        wb_bf = keep.tile([P, PACK * N], BF16, name="wb_bf", align_bytes=64)
+        wb_codes = keep.tile([P, N], U32, name="wb_codes", align_bytes=64)
+        wb_sc = keep.tile([P, N], U8, name="wb_sc", align_bytes=64)
+        res_sb = [keep.tile([P, PACK, HALF], F32, name=f"res{h}") for h in range(2)]
+        xg = keep.tile([P, PACK, J], F32, name="xg")
+        zg = keep.tile([P, PACK, J], F32, name="zg")
+        x_codes = keep.tile([P, J], U32, name="x_codes", align_bytes=64)
+        x_sc = keep.tile([P, J], U8, name="x_sc", align_bytes=64)
+        z_codes = keep.tile([P, J], U32, name="z_codes", align_bytes=64)
+        z_sc = keep.tile([P, J], U8, name="z_sc", align_bytes=64)
+        gate = [keep.tile([P, PACK, CHUNK], F32, name=f"gate{c}") for c in range(CHUNKS)]
+        o_codes = keep.tile([P, J], U32, name="o_codes", align_bytes=64)
+        o_sc = keep.tile([P, J], U8, name="o_sc", align_bytes=64)
+        warm = keep.tile([P, 2], F32, name="warm")
+
+        x_rows = xT.rearrange("(p t) j -> t p j", t=PACK)
+        z_rows = zT.rearrange("(p t) j -> t p j", t=PACK)
+        res_rows = res.rearrange("(p t) j -> p t j", t=PACK)
+        out_rows = out_0.rearrange("(p t) j -> p t j", t=PACK)
+        out_words = out_1[0].rearrange("p j i -> p (j i)").bitcast(I32)
+
+        nc.vector.memset(wa_sraw[:].bitcast(I32), 0)
+        nc.vector.memset(warm[:, 0:1], 0.0)
+        nc.scalar.activation(out=warm[:, 1:2], in_=warm[:, 0:1], func=SIGMOID)
+
+        nc.sync.dma_start(z_list[:], offs2)
+        nc.sync.dma_start(out=wa_raw[:].bitcast(I32), in_=wa_words[0].bitcast(I32))
+        nc.sync.dma_start(out=z_planes[0][:], in_=z_rows[0])
+        nc.sync.dma_start(out=z_wgt[:], in_=wgt2)
+        for q in range(4):
+            nc.gpsimd.dma_start(
+                out=wa_sraw[32 * q : 32 * q + 4, :].bitcast(I32), in_=wa_scales[0, 4 * q : 4 * q + 4, :].bitcast(I32)
+            )
+        for t in range(1, PACK):
+            nc.sync.dma_start(out=z_planes[t][:], in_=z_rows[t])
+        nc.sync.dma_start(out=wb_raw[:], in_=wb.rearrange("(p t) n -> p t n", t=PACK))
+        nc.sync.dma_start(x_list[:], offs)
+        nc.sync.dma_start(out=x_planes[0][:], in_=x_rows[0])
+        nc.sync.dma_start(out=x_wgt[:], in_=wgt)
+        for t in range(1, PACK):
+            nc.sync.dma_start(out=x_planes[t][:], in_=x_rows[t])
+        for h in range(2):
+            nc.sync.dma_start(out=res_sb[h][:], in_=res_rows[:, :, h * HALF : (h + 1) * HALF])
+
+        nc.vector.tensor_copy(
+            out=wa_codes[:].rearrange("p (t m b) -> p m t b", t=PACK, b=2),
+            in_=wa_raw[:].rearrange("p (m t b) -> p m t b", t=PACK, b=2),
+        )
+        nc.vector.tensor_copy(
+            out=wa_sc[:].rearrange("p (t m) -> p m t", t=PACK), in_=wa_sraw[:].rearrange("p (m t) -> p m t", t=PACK)
+        )
+
+        def gather(dst, planes, lst, weights, t, c0, c1):
+            nc.vector.tensor_tensor(
+                dst[:, t, c0:c1], planes[t][:].indirect(lst[:, c0 // 16 : c1 // 16]), weights[:, c0:c1], MULT
+            )
+
+        def quantise(codes, scales, bf, c0, c1):
+            nc.vector.quantize_mx(
+                out=codes[:, c0:c1].bitcast(E4M3), scales=scales[:, c0:c1], in_=bf[:].rearrange("p j t -> p (j t)")
+            )
+
+        def rounded(src, tag):
+            bf = ring.tile([P, CHUNK, PACK], BF16, name=tag, tag=tag, align_bytes=64, bufs=4)
+            interleave(nc.scalar.copy, bf[:], src)
+            return bf
+
+        def products(w_codes, w_sc, codes, scales, c0, c1):
+            banks = []
+            for pair in range(2):
+                bank = psum.tile([P, 2, CHUNK], F32, name="bank", tag="bank")
+                for u in range(2):
+                    t = 2 * pair + u
+                    nc.tensor.matmul_mx(
+                        out=bank[:, u, :],
+                        lhsT=w_codes(t),
+                        lhsT_scale=w_sc[:, t * P : (t + 1) * P],
+                        rhs=codes[:, c0:c1].bitcast(E4M3),
+                        rhs_scale=scales[:, c0:c1],
+                        start=True,
+                        stop=True,
+                    )
+                banks.append(bank)
+            return banks
+
+        def wb_cols(t):
+            return wb_codes[:, t * P : (t + 1) * P].bitcast(E4M3)
+
+        def wa_cols(t):
+            return wa_codes[:, 2 * t * P : 2 * (t + 1) * P].bitcast(E2M1)
+
+        spans = [(c * CHUNK, (c + 1) * CHUNK) for c in range(CHUNKS)]
+
+        for t in range(PACK - 1):
+            gather(zg, z_planes, z_list, z_wgt, t, 0, J)
+        for c0, c1 in spans:
+            gather(zg, z_planes, z_list, z_wgt, PACK - 1, c0, c1)
+
+        z_bf = [rounded(zg[:, :, c0:c1], "z_bf") for c0, c1 in spans[:1]]
+        nc.scalar.copy(
+            out=wb_bf[:].rearrange("p (t m i) -> p m i t", t=PACK, i=PACK),
+            in_=wb_raw[:].rearrange("p i (m t) -> p m i t", t=PACK),
+        )
+        quantise(z_codes, z_sc, z_bf[0], *spans[0])
+        gather(xg, x_planes, x_list, x_wgt, 0, 0, J)
+        nc.vector.quantize_mx(out=wb_codes[:].bitcast(E4M3), scales=wb_sc[:], in_=wb_bf[:])
+        for c, (c0, c1) in enumerate(spans):
+            if c > 0:
+                quantise(z_codes, z_sc, rounded(zg[:, :, c0:c1], "z_bf"), c0, c1)
+            banks = products(wb_cols, wb_sc, z_codes, z_sc, c0, c1)
+            for pair in range(2):
+                nc.scalar.activation(out=gate[c][:, 2 * pair : 2 * pair + 2, :], in_=banks[pair][:], func=SIGMOID)
+            if c in (1, 3):
+                gather(xg, x_planes, x_list, x_wgt, 1 + c // 2, 0, J)
+
+        for c0, c1 in spans:
+            gather(xg, x_planes, x_list, x_wgt, PACK - 1, c0, c1)
+
+        def front(c):
+            c0, c1 = spans[c]
+            quantise(x_codes, x_sc, rounded(xg[:, :, c0:c1], "x_bf"), c0, c1)
+            return products(wa_cols, wa_sc, x_codes, x_sc, c0, c1)
+
+        def middle(c, banks):
+            c0, c1 = spans[c]
+            prod = ring.tile([P, PACK, CHUNK], F32, name="prod", tag="prod")
+            for pair in range(2):
+                rows = slice(2 * pair, 2 * pair + 2)
+                nc.vector.tensor_tensor(prod[:, rows, :], banks[pair][:], gate[c][:, rows, :], MULT)
+            return prod
+
+        def summed(c, prod):
+            c0, c1 = spans[c]
+            h = c0 // HALF
+            o = ring.tile([P, PACK, CHUNK], F32, name="o", tag="o", bufs=3)
+            nc.vector.tensor_tensor(o[:], prod[:], res_sb[h][:, :, c0 - h * HALF : c1 - h * HALF], ADD)
+            nc.sync.dma_start(out=out_rows[:, :, c0:c1], in_=o[:])
+            return rounded(o[:], "o_bf")
+
+        def planes(c, bf):
+            c0, c1 = spans[c]
+            quantise(o_codes, o_sc, bf, c0, c1)
+            nc.sync.dma_start(out=out_words[:, c0:c1], in_=o_codes[:, c0:c1].bitcast(I32))
+
+        banks = {0: front(0), 1: front(1)}
+        done = {}
+        for c in range(CHUNKS):
+            prod = middle(c, banks[c])
+            if c + 2 < CHUNKS:
+                banks[c + 2] = front(c + 2)
+            if c >= 1:
+                planes(c - 1, done[c - 1])
+            done[c] = summed(c, prod)
+        planes(CHUNKS - 1, done[CHUNKS - 1])
+        for q in range(4):
+            queue = nc.sync if q % 2 == 0 else nc.scalar
+            queue.dma_start(
+                out=out_2[0, 4 * q : 4 * q + 4, :].bitcast(I32), in_=o_sc[32 * q : 32 * q + 4, :].bitcast(I32)
+            )

@@ -1,6 +1,7 @@
 from contextlib import ExitStack
 
 import concourse.mybir as mybir
+from concourse.masks import make_identity
 
 K, N, T, J = 512, 512, 2048, 1024
 FLOPS = 2 * 2 * K * N * J
@@ -19,9 +20,12 @@ SIGMOID = mybir.ActivationFunctionType.Sigmoid
 
 P = 128
 PACK = 4
-CHUNK = 256
-CHUNKS = J // CHUNK
+BANK = 512
+HEADS = 8
 HALF = J // 2
+WIDTHS = [128,256,256,256,128]
+WORD_CUTS = [0,384,896,1024]
+RES_CUTS = [0,384,1024]
 
 
 def interleave(engine_copy, dst, src):
@@ -32,6 +36,12 @@ def tile_list_gate_resP_kernel(
     tc, xT, wgt, zT, wgt2, wa_words, wa_scales, wb, res, offs, offs2, out_0, out_1, out_2
 ):
     nc = tc.nc
+    spans = []
+    for w in WIDTHS:
+        start = spans[-1][1] if spans else 0
+        spans.append((start, start + w))
+    chunks = len(spans)
+
     with ExitStack() as ctx:
         keep = ctx.enter_context(tc.tile_pool(name="keep", bufs=1))
         ring = ctx.enter_context(tc.tile_pool(name="ring", bufs=2))
@@ -41,6 +51,8 @@ def tile_list_gate_resP_kernel(
         z_list = keep.tile([P, J // 16], U16, name="z_list")
         x_planes = [keep.tile([P, T], F32, name=f"x_plane{t}") for t in range(PACK)]
         z_planes = [keep.tile([P, T], F32, name=f"z_plane{t}") for t in range(PACK)]
+        ident = keep.tile([P, P], F32, name="ident")
+        head_rows = keep.tile([P, HALF], F32, name="head_rows")
         x_wgt = keep.tile([P, J], F32, name="x_wgt")
         z_wgt = keep.tile([P, J], F32, name="z_wgt")
         wa_raw = keep.tile([P, 2 * N], U8, name="wa_raw", align_bytes=64)
@@ -51,14 +63,15 @@ def tile_list_gate_resP_kernel(
         wb_bf = keep.tile([P, PACK * N], BF16, name="wb_bf", align_bytes=64)
         wb_codes = keep.tile([P, N], U32, name="wb_codes", align_bytes=64)
         wb_sc = keep.tile([P, N], U8, name="wb_sc", align_bytes=64)
-        res_sb = [keep.tile([P, PACK, HALF], F32, name=f"res{h}") for h in range(2)]
+        res_spans = list(zip(RES_CUTS[:-1], RES_CUTS[1:]))
+        res_sb = [keep.tile([P, PACK, b - a], F32, name=f"res{a}") for a, b in res_spans]
         xg = keep.tile([P, PACK, J], F32, name="xg")
         zg = keep.tile([P, PACK, J], F32, name="zg")
         x_codes = keep.tile([P, J], U32, name="x_codes", align_bytes=64)
         x_sc = keep.tile([P, J], U8, name="x_sc", align_bytes=64)
         z_codes = keep.tile([P, J], U32, name="z_codes", align_bytes=64)
         z_sc = keep.tile([P, J], U8, name="z_sc", align_bytes=64)
-        gate = [keep.tile([P, PACK, CHUNK], F32, name=f"gate{c}") for c in range(CHUNKS)]
+        gate = [keep.tile([P, PACK, w], F32, name=f"gate{c}") for c, w in enumerate(WIDTHS)]
         o_codes = keep.tile([P, J], U32, name="o_codes", align_bytes=64)
         o_sc = keep.tile([P, J], U8, name="o_sc", align_bytes=64)
         warm = keep.tile([P, 2], F32, name="warm")
@@ -69,28 +82,52 @@ def tile_list_gate_resP_kernel(
         out_rows = out_0.rearrange("(p t) j -> p t j", t=PACK)
         out_words = out_1[0].rearrange("p j i -> p (j i)").bitcast(I32)
 
-        nc.vector.memset(wa_sraw[:].bitcast(I32), 0)
+        def half_rows(w):
+            stride = 7 * J + HALF
+            flat = w.rearrange("p j -> (p j)")[7 * J : 7 * J + 2 * HEADS * stride]
+            return flat.rearrange("(q s) -> q s", s=stride)[:, :HALF]
+
+        nc.gpsimd.memset(wa_sraw[:].bitcast(I32), 0)
+        nc.vector.memset(head_rows[32:64, :], 0.0)
+        nc.vector.memset(head_rows[64:128, :], 0.0)
         nc.vector.memset(warm[:, 0:1], 0.0)
-        nc.scalar.activation(out=warm[:, 1:2], in_=warm[:, 0:1], func=SIGMOID)
+        make_identity(nc, ident[:])
 
         nc.sync.dma_start(z_list[:], offs2)
-        nc.sync.dma_start(out=wa_raw[:].bitcast(I32), in_=wa_words[0].bitcast(I32))
-        nc.sync.dma_start(out=z_planes[0][:], in_=z_rows[0])
-        nc.sync.dma_start(out=z_wgt[:], in_=wgt2)
+        nc.sync.dma_start(out=head_rows[0:16, :], in_=half_rows(wgt2))
+        nc.sync.dma_start(out=head_rows[16:32, :], in_=half_rows(wgt))
         for q in range(4):
-            nc.gpsimd.dma_start(
+            nc.sync.dma_start(
                 out=wa_sraw[32 * q : 32 * q + 4, :].bitcast(I32), in_=wa_scales[0, 4 * q : 4 * q + 4, :].bitcast(I32)
             )
+        nc.sync.dma_start(out=wa_raw[:].bitcast(I32), in_=wa_words[0].bitcast(I32))
+        nc.sync.dma_start(out=z_planes[0][:], in_=z_rows[0])
+        nc.scalar.activation(out=warm[:, 1:2], in_=warm[:, 0:1], func=SIGMOID)
         for t in range(1, PACK):
             nc.sync.dma_start(out=z_planes[t][:], in_=z_rows[t])
-        nc.sync.dma_start(out=wb_raw[:], in_=wb.rearrange("(p t) n -> p t n", t=PACK))
         nc.sync.dma_start(x_list[:], offs)
-        nc.sync.dma_start(out=x_planes[0][:], in_=x_rows[0])
-        nc.sync.dma_start(out=x_wgt[:], in_=wgt)
-        for t in range(1, PACK):
+        for t in range(PACK):
+            if t == 0:
+                nc.sync.dma_start(out=wb_raw[:], in_=wb.rearrange("(p t) n -> p t n", t=PACK))
             nc.sync.dma_start(out=x_planes[t][:], in_=x_rows[t])
-        for h in range(2):
-            nc.sync.dma_start(out=res_sb[h][:], in_=res_rows[:, :, h * HALF : (h + 1) * HALF])
+        for (a, b), tile in zip(res_spans, res_sb):
+            nc.sync.dma_start(out=tile[:], in_=res_rows[:, :, a:b])
+
+        turned = psum.tile([P, PACK, P], F32, name="bank", tag="bank")
+        for c in range(PACK):
+            nc.tensor.transpose(turned[:, c, :], head_rows[:, c * P : (c + 1) * P], ident[:])
+        for s, weights in enumerate((z_wgt, x_wgt)):
+            for e in range(2):
+                spread = ring.tile([P, PACK, HEADS, 16], F32, name="spread", tag="spread")
+                first = 16 * s + e
+                nc.scalar.copy(
+                    out=spread[:],
+                    in_=turned[:, :, first : first + 15 : 2].unsqueeze(3).to_broadcast([P, PACK, HEADS, 16]),
+                )
+                back = psum.tile([P, PACK, P], F32, name="bank", tag="bank")
+                for c in range(PACK):
+                    nc.tensor.transpose(back[:, c, :], spread[:, c].rearrange("p g r -> p (g r)"), ident[:])
+                nc.scalar.copy(out=weights[:, e * HALF : (e + 1) * HALF], in_=back[:].rearrange("p c j -> p (c j)"))
 
         nc.vector.tensor_copy(
             out=wa_codes[:].rearrange("p (t m b) -> p m t b", t=PACK, b=2),
@@ -110,17 +147,18 @@ def tile_list_gate_resP_kernel(
                 out=codes[:, c0:c1].bitcast(E4M3), scales=scales[:, c0:c1], in_=bf[:].rearrange("p j t -> p (j t)")
             )
 
-        def rounded(src, tag):
-            bf = ring.tile([P, CHUNK, PACK], BF16, name=tag, tag=tag, align_bytes=64, bufs=4)
-            interleave(nc.scalar.copy, bf[:], src)
+        def rounded(src, tag, copy=nc.scalar.copy):
+            bf = ring.tile([P, src.shape[2], PACK], BF16, name=tag, tag=tag, align_bytes=64, bufs=4)
+            interleave(copy, bf[:], src)
             return bf
 
         def products(w_codes, w_sc, codes, scales, c0, c1):
+            per_bank = min(PACK, BANK // (c1 - c0))
             banks = []
-            for pair in range(2):
-                bank = psum.tile([P, 2, CHUNK], F32, name="bank", tag="bank")
-                for u in range(2):
-                    t = 2 * pair + u
+            for t0 in range(0, PACK, per_bank):
+                bank = psum.tile([P, per_bank, c1 - c0], F32, name="bank", tag="bank")
+                for u in range(per_bank):
+                    t = t0 + u
                     nc.tensor.matmul_mx(
                         out=bank[:, u, :],
                         lhsT=w_codes(t),
@@ -130,7 +168,7 @@ def tile_list_gate_resP_kernel(
                         start=True,
                         stop=True,
                     )
-                banks.append(bank)
+                banks.append((slice(t0, t0 + per_bank), bank))
             return banks
 
         def wb_cols(t):
@@ -139,69 +177,77 @@ def tile_list_gate_resP_kernel(
         def wa_cols(t):
             return wa_codes[:, 2 * t * P : 2 * (t + 1) * P].bitcast(E2M1)
 
-        spans = [(c * CHUNK, (c + 1) * CHUNK) for c in range(CHUNKS)]
-
-        for t in range(PACK - 1):
+        for e in range(2):
+            gather(zg, z_planes, z_list, z_wgt, 0, e * HALF, (e + 1) * HALF)
+        for t in range(1, PACK - 1):
             gather(zg, z_planes, z_list, z_wgt, t, 0, J)
         for c0, c1 in spans:
             gather(zg, z_planes, z_list, z_wgt, PACK - 1, c0, c1)
-
-        z_bf = [rounded(zg[:, :, c0:c1], "z_bf") for c0, c1 in spans[:1]]
-        nc.scalar.copy(
-            out=wb_bf[:].rearrange("p (t m i) -> p m i t", t=PACK, i=PACK),
-            in_=wb_raw[:].rearrange("p i (m t) -> p m i t", t=PACK),
-        )
-        quantise(z_codes, z_sc, z_bf[0], *spans[0])
         gather(xg, x_planes, x_list, x_wgt, 0, 0, J)
-        nc.vector.quantize_mx(out=wb_codes[:].bitcast(E4M3), scales=wb_sc[:], in_=wb_bf[:])
-        for c, (c0, c1) in enumerate(spans):
-            if c > 0:
-                quantise(z_codes, z_sc, rounded(zg[:, :, c0:c1], "z_bf"), c0, c1)
-            banks = products(wb_cols, wb_sc, z_codes, z_sc, c0, c1)
-            for pair in range(2):
-                nc.scalar.activation(out=gate[c][:, 2 * pair : 2 * pair + 2, :], in_=banks[pair][:], func=SIGMOID)
-            if c in (1, 3):
-                gather(xg, x_planes, x_list, x_wgt, 1 + c // 2, 0, J)
 
-        for c0, c1 in spans:
-            gather(xg, x_planes, x_list, x_wgt, PACK - 1, c0, c1)
+        for c, (c0, c1) in enumerate(spans):
+            if c == 1:
+                nc.scalar.copy(
+                    out=wb_bf[:].rearrange("p (t m i) -> p m i t", t=PACK, i=PACK),
+                    in_=wb_raw[:].rearrange("p i (m t) -> p m i t", t=PACK),
+                )
+                nc.vector.quantize_mx(out=wb_codes[:].bitcast(E4M3), scales=wb_sc[:], in_=wb_bf[:])
+            quantise(z_codes, z_sc, rounded(zg[:, :, c0:c1], "z_bf"), c0, c1)
+        for t in (1, 2):
+            gather(xg, x_planes, x_list, x_wgt, t, 0, J)
+
+        def gated(c):
+            c0, c1 = spans[c]
+            for rows, bank in products(wb_cols, wb_sc, z_codes, z_sc, c0, c1):
+                nc.scalar.activation(out=gate[c][:, rows, :], in_=bank[:], func=SIGMOID)
 
         def front(c):
             c0, c1 = spans[c]
             quantise(x_codes, x_sc, rounded(xg[:, :, c0:c1], "x_bf"), c0, c1)
             return products(wa_cols, wa_sc, x_codes, x_sc, c0, c1)
 
-        def middle(c, banks):
+        def combined(c, banks):
             c0, c1 = spans[c]
-            prod = ring.tile([P, PACK, CHUNK], F32, name="prod", tag="prod")
-            for pair in range(2):
-                rows = slice(2 * pair, 2 * pair + 2)
-                nc.vector.tensor_tensor(prod[:, rows, :], banks[pair][:], gate[c][:, rows, :], MULT)
-            return prod
-
-        def summed(c, prod):
-            c0, c1 = spans[c]
-            h = c0 // HALF
-            o = ring.tile([P, PACK, CHUNK], F32, name="o", tag="o", bufs=3)
-            nc.vector.tensor_tensor(o[:], prod[:], res_sb[h][:, :, c0 - h * HALF : c1 - h * HALF], ADD)
+            h = [a <= c0 < b for a, b in res_spans].index(True)
+            a = res_spans[h][0]
+            prod = ring.tile([P, PACK, c1 - c0], F32, name="prod", tag="prod", bufs=1)
+            o = ring.tile([P, PACK, c1 - c0], F32, name="o", tag="o", bufs=3)
+            pairs = (slice(0, 2), slice(2, 4))
+            for k, rows in enumerate(pairs):
+                ya = banks[k][1][:] if len(banks) == 2 else banks[0][1][:, rows, :]
+                nc.vector.tensor_tensor(prod[:, rows, :], ya, gate[c][:, rows, :], MULT)
+            for rows in pairs:
+                nc.vector.tensor_tensor(o[:, rows, :], prod[:, rows, :], res_sb[h][:, rows, c0 - a : c1 - a], ADD)
             nc.sync.dma_start(out=out_rows[:, :, c0:c1], in_=o[:])
             return rounded(o[:], "o_bf")
 
         def planes(c, bf):
             c0, c1 = spans[c]
             quantise(o_codes, o_sc, bf, c0, c1)
-            nc.sync.dma_start(out=out_words[:, c0:c1], in_=o_codes[:, c0:c1].bitcast(I32))
+            if c1 in WORD_CUTS:
+                a = WORD_CUTS[WORD_CUTS.index(c1) - 1]
+                nc.sync.dma_start(out=out_words[:, a:c1], in_=o_codes[:, a:c1].bitcast(I32))
 
-        banks = {0: front(0), 1: front(1)}
+        for c in range(5):
+            gated(c)
+        for c0, c1 in spans:
+            gather(xg, x_planes, x_list, x_wgt, PACK - 1, c0, c1)
+        banks = {}
+        for c in range(2):
+            banks[c] = front(c)
+            if 5 + c < chunks:
+                gated(5 + c)
+        for c in range(5 + 2, chunks):
+            gated(c)
         done = {}
-        for c in range(CHUNKS):
-            prod = middle(c, banks[c])
-            if c + 2 < CHUNKS:
+        for c in range(chunks):
+            if c + 2 < chunks:
                 banks[c + 2] = front(c + 2)
-            if c >= 1:
-                planes(c - 1, done[c - 1])
-            done[c] = summed(c, prod)
-        planes(CHUNKS - 1, done[CHUNKS - 1])
+            if c >= 2:
+                planes(c - 2, done[c - 2])
+            done[c] = combined(c, banks[c])
+        for c in range(chunks - 2, chunks):
+            planes(c, done[c])
         for q in range(4):
             queue = nc.sync if q % 2 == 0 else nc.scalar
             queue.dma_start(

@@ -65,7 +65,8 @@ def tile_list_gate_resP_kernel(
         wb_sc = keep.tile([P, N], U8, name="wb_sc", align_bytes=64)
         res_spans = list(zip(RES_CUTS[:-1], RES_CUTS[1:]))
         res_sb = [keep.tile([P, PACK, b - a], F32, name=f"res{a}") for a, b in res_spans]
-        xg = keep.tile([P, PACK, J], F32, name="xg")
+        xg_flat = keep.tile([P, PACK * J], F32, name="xg", align_bytes=64)
+        xg = xg_flat[:].rearrange("p (t j) -> p t j", t=PACK)
         zg = keep.tile([P, PACK, J], F32, name="zg")
         x_codes = keep.tile([P, J], U32, name="x_codes", align_bytes=64)
         x_sc = keep.tile([P, J], U8, name="x_sc", align_bytes=64)
@@ -93,7 +94,6 @@ def tile_list_gate_resP_kernel(
         nc.vector.memset(warm[:, 0:1], 0.0)
         make_identity(nc, ident[:])
 
-        nc.sync.dma_start(z_list[:], offs2)
         nc.sync.dma_start(out=head_rows[0:16, :], in_=half_rows(wgt2))
         nc.sync.dma_start(out=head_rows[16:32, :], in_=half_rows(wgt))
         for q in range(4):
@@ -101,14 +101,14 @@ def tile_list_gate_resP_kernel(
                 out=wa_sraw[32 * q : 32 * q + 4, :].bitcast(I32), in_=wa_scales[0, 4 * q : 4 * q + 4, :].bitcast(I32)
             )
         nc.sync.dma_start(out=wa_raw[:].bitcast(I32), in_=wa_words[0].bitcast(I32))
+        nc.sync.dma_start(out=wb_raw[:], in_=wb.rearrange("(p t) n -> p t n", t=PACK))
+        nc.sync.dma_start(z_list[:], offs2)
         nc.sync.dma_start(out=z_planes[0][:], in_=z_rows[0])
         nc.scalar.activation(out=warm[:, 1:2], in_=warm[:, 0:1], func=SIGMOID)
         for t in range(1, PACK):
             nc.sync.dma_start(out=z_planes[t][:], in_=z_rows[t])
         nc.sync.dma_start(x_list[:], offs)
         for t in range(PACK):
-            if t == 0:
-                nc.sync.dma_start(out=wb_raw[:], in_=wb.rearrange("(p t) n -> p t n", t=PACK))
             nc.sync.dma_start(out=x_planes[t][:], in_=x_rows[t])
         for (a, b), tile in zip(res_spans, res_sb):
             nc.sync.dma_start(out=tile[:], in_=res_rows[:, :, a:b])
@@ -136,6 +136,11 @@ def tile_list_gate_resP_kernel(
         nc.vector.tensor_copy(
             out=wa_sc[:].rearrange("p (t m) -> p m t", t=PACK), in_=wa_sraw[:].rearrange("p (m t) -> p m t", t=PACK)
         )
+        nc.vector.tensor_copy(
+            out=wb_bf[:].rearrange("p (t m i) -> p m i t", t=PACK, i=PACK),
+            in_=wb_raw[:].rearrange("p i (m t) -> p m i t", t=PACK),
+        )
+        nc.vector.quantize_mx(out=wb_codes[:].bitcast(E4M3), scales=wb_sc[:], in_=wb_bf[:])
 
         def gather(dst, planes, lst, weights, t, c0, c1):
             nc.vector.tensor_tensor(
@@ -185,16 +190,6 @@ def tile_list_gate_resP_kernel(
             gather(zg, z_planes, z_list, z_wgt, PACK - 1, c0, c1)
         gather(xg, x_planes, x_list, x_wgt, 0, 0, J)
 
-        for c, (c0, c1) in enumerate(spans):
-            if c == 1:
-                nc.scalar.copy(
-                    out=wb_bf[:].rearrange("p (t m i) -> p m i t", t=PACK, i=PACK),
-                    in_=wb_raw[:].rearrange("p i (m t) -> p m i t", t=PACK),
-                )
-                nc.vector.quantize_mx(out=wb_codes[:].bitcast(E4M3), scales=wb_sc[:], in_=wb_bf[:])
-            quantise(z_codes, z_sc, rounded(zg[:, :, c0:c1], "z_bf"), c0, c1)
-        for t in (1, 2):
-            gather(xg, x_planes, x_list, x_wgt, t, 0, J)
 
         def gated(c):
             c0, c1 = spans[c]
@@ -228,17 +223,21 @@ def tile_list_gate_resP_kernel(
                 a = WORD_CUTS[WORD_CUTS.index(c1) - 1]
                 nc.sync.dma_start(out=out_words[:, a:c1], in_=o_codes[:, a:c1].bitcast(I32))
 
-        for c in range(5):
+        for c, (c0, c1) in enumerate(spans):
+            quantise(z_codes, z_sc, rounded(zg[:, :, c0:c1], "z_bf"), c0, c1)
+        for c in range(chunks):
             gated(c)
-        for c0, c1 in spans:
+        for t in (1, 2):
+            gather(xg, x_planes, x_list, x_wgt, t, 0, J)
+        for c0, c1 in spans[:3]:
             gather(xg, x_planes, x_list, x_wgt, PACK - 1, c0, c1)
-        banks = {}
-        for c in range(2):
-            banks[c] = front(c)
-            if 5 + c < chunks:
-                gated(5 + c)
-        for c in range(5 + 2, chunks):
-            gated(c)
+        lent = xg[:, PACK - 1, spans[3][0] : spans[3][1]].bitcast(BF16).rearrange("p (j t) -> p j t", t=PACK)
+        interleave(nc.scalar.copy, lent, xg[:, :, spans[0][0] : spans[0][1]])
+        quantise(x_codes, x_sc, lent, *spans[0])
+        banks = {0: products(wa_cols, wa_sc, x_codes, x_sc, *spans[0])}
+        for c0, c1 in spans[3:]:
+            gather(xg, x_planes, x_list, x_wgt, PACK - 1, c0, c1)
+        banks[1] = front(1)
         done = {}
         for c in range(chunks):
             if c + 2 < chunks:

@@ -19,38 +19,41 @@ ADD = mybir.AluOpType.add
 SIGMOID = mybir.ActivationFunctionType.Sigmoid
 
 P = 128
-PACK = 4
+SLOTS = 4
 BANK = 512
 HEADS = 8
+GROUP = 16
 HALF = J // 2
-WIDTHS = [128,256,256,256,128]
-WORD_CUTS = [0,384,896,1024]
-RES_CUTS = [0,384,1024]
+
+CHUNK_CUTS = [0, 128, 384, 640, 896, 1024]
+Z_GATHER_CUTS = [0, 384, 1024]
+X_GATHER_CUTS = [0, 128, 640, 1024]
+RES_CUTS = [0, 384, 1024]
+WORD_CUTS = [0, 384, 896, 1024]
+AHEAD = 256
+BEHIND = 2
 
 
-def interleave(engine_copy, dst, src):
-    engine_copy(out=dst.rearrange("p (c i) t -> p c t i", i=4), in_=src.rearrange("p t (c i) -> p c t i", i=4))
+def spans_of(cuts):
+    return list(zip(cuts[:-1], cuts[1:]))
 
 
 def tile_list_gate_resP_kernel(
     tc, xT, wgt, zT, wgt2, wa_words, wa_scales, wb, res, offs, offs2, out_0, out_1, out_2
 ):
     nc = tc.nc
-    spans = []
-    for w in WIDTHS:
-        start = spans[-1][1] if spans else 0
-        spans.append((start, start + w))
-    chunks = len(spans)
+    chunks = spans_of(CHUNK_CUTS)
+    res_spans = spans_of(RES_CUTS)
 
     with ExitStack() as ctx:
         keep = ctx.enter_context(tc.tile_pool(name="keep", bufs=1))
         ring = ctx.enter_context(tc.tile_pool(name="ring", bufs=2))
         psum = ctx.enter_context(tc.psum_pool(name="psum", bufs=8))
 
-        x_list = keep.tile([P, J // 16], U16, name="x_list")
-        z_list = keep.tile([P, J // 16], U16, name="z_list")
-        x_planes = [keep.tile([P, T], F32, name=f"x_plane{t}") for t in range(PACK)]
-        z_planes = [keep.tile([P, T], F32, name=f"z_plane{t}") for t in range(PACK)]
+        x_list = keep.tile([P, J // GROUP], U16, name="x_list")
+        z_list = keep.tile([P, J // GROUP], U16, name="z_list")
+        x_planes = [keep.tile([P, T], F32, name=f"x_plane{t}") for t in range(SLOTS)]
+        z_planes = [keep.tile([P, T], F32, name=f"z_plane{t}") for t in range(SLOTS)]
         ident = keep.tile([P, P], F32, name="ident")
         head_rows = keep.tile([P, HALF], F32, name="head_rows")
         x_wgt = keep.tile([P, J], F32, name="x_wgt")
@@ -59,114 +62,117 @@ def tile_list_gate_resP_kernel(
         wa_sraw = keep.tile([P, N], U8, name="wa_sraw", align_bytes=64)
         wa_codes = keep.tile([P, 2 * N], U8, name="wa_codes", align_bytes=64)
         wa_sc = keep.tile([P, N], U8, name="wa_sc", align_bytes=64)
-        wb_raw = keep.tile([P, PACK, N], F32, name="wb_raw")
-        wb_bf = keep.tile([P, PACK * N], BF16, name="wb_bf", align_bytes=64)
+        wb_raw = keep.tile([P, SLOTS, N], F32, name="wb_raw")
+        wb_bf = keep.tile([P, SLOTS * N], BF16, name="wb_bf", align_bytes=64)
         wb_codes = keep.tile([P, N], U32, name="wb_codes", align_bytes=64)
         wb_sc = keep.tile([P, N], U8, name="wb_sc", align_bytes=64)
-        res_spans = list(zip(RES_CUTS[:-1], RES_CUTS[1:]))
-        res_sb = [keep.tile([P, PACK, b - a], F32, name=f"res{a}") for a, b in res_spans]
-        xg_flat = keep.tile([P, PACK * J], F32, name="xg", align_bytes=64)
-        xg = xg_flat[:].rearrange("p (t j) -> p t j", t=PACK)
-        zg = keep.tile([P, PACK, J], F32, name="zg")
+        res_sb = [keep.tile([P, SLOTS, b - a], F32, name=f"res{a}") for a, b in res_spans]
+        xg_flat = keep.tile([P, SLOTS * J], F32, name="xg", align_bytes=64)
+        xg = xg_flat[:].rearrange("p (t j) -> p t j", t=SLOTS)
+        zg = keep.tile([P, SLOTS, J], F32, name="zg")
         x_codes = keep.tile([P, J], U32, name="x_codes", align_bytes=64)
         x_sc = keep.tile([P, J], U8, name="x_sc", align_bytes=64)
         z_codes = keep.tile([P, J], U32, name="z_codes", align_bytes=64)
         z_sc = keep.tile([P, J], U8, name="z_sc", align_bytes=64)
-        gate = [keep.tile([P, PACK, w], F32, name=f"gate{c}") for c, w in enumerate(WIDTHS)]
+        gate = [keep.tile([P, SLOTS, b - a], F32, name=f"gate{a}") for a, b in chunks]
         o_codes = keep.tile([P, J], U32, name="o_codes", align_bytes=64)
         o_sc = keep.tile([P, J], U8, name="o_sc", align_bytes=64)
-        warm = keep.tile([P, 2], F32, name="warm")
 
-        x_rows = xT.rearrange("(p t) j -> t p j", t=PACK)
-        z_rows = zT.rearrange("(p t) j -> t p j", t=PACK)
-        res_rows = res.rearrange("(p t) j -> p t j", t=PACK)
-        out_rows = out_0.rearrange("(p t) j -> p t j", t=PACK)
+        x_rows = xT.rearrange("(p t) j -> t p j", t=SLOTS)
+        z_rows = zT.rearrange("(p t) j -> t p j", t=SLOTS)
+        res_rows = res.rearrange("(p t) j -> p t j", t=SLOTS)
+        out_rows = out_0.rearrange("(p t) j -> p t j", t=SLOTS)
         out_words = out_1[0].rearrange("p j i -> p (j i)").bitcast(I32)
 
         def half_rows(w):
-            stride = 7 * J + HALF
-            flat = w.rearrange("p j -> (p j)")[7 * J : 7 * J + 2 * HEADS * stride]
-            return flat.rearrange("(q s) -> q s", s=stride)[:, :HALF]
+            step = 7 * J + HALF
+            flat = w.rearrange("p j -> (p j)")[7 * J : 7 * J + 2 * HEADS * step]
+            return flat.rearrange("(q s) -> q s", s=step)[:, :HALF]
 
         nc.gpsimd.memset(wa_sraw[:].bitcast(I32), 0)
         nc.vector.memset(head_rows[32:64, :], 0.0)
         nc.vector.memset(head_rows[64:128, :], 0.0)
-        nc.vector.memset(warm[:, 0:1], 0.0)
         make_identity(nc, ident[:])
 
         nc.sync.dma_start(out=head_rows[0:16, :], in_=half_rows(wgt2))
         nc.sync.dma_start(out=head_rows[16:32, :], in_=half_rows(wgt))
         for q in range(4):
-            nc.sync.dma_start(
+            nc.scalar.dma_start(
                 out=wa_sraw[32 * q : 32 * q + 4, :].bitcast(I32), in_=wa_scales[0, 4 * q : 4 * q + 4, :].bitcast(I32)
             )
         nc.sync.dma_start(out=wa_raw[:].bitcast(I32), in_=wa_words[0].bitcast(I32))
-        nc.sync.dma_start(out=wb_raw[:], in_=wb.rearrange("(p t) n -> p t n", t=PACK))
+        nc.sync.dma_start(out=wb_raw[:], in_=wb.rearrange("(p t) n -> p t n", t=SLOTS))
         nc.sync.dma_start(z_list[:], offs2)
-        nc.sync.dma_start(out=z_planes[0][:], in_=z_rows[0])
-        nc.scalar.activation(out=warm[:, 1:2], in_=warm[:, 0:1], func=SIGMOID)
-        for t in range(1, PACK):
+        for t in range(SLOTS):
             nc.sync.dma_start(out=z_planes[t][:], in_=z_rows[t])
         nc.sync.dma_start(x_list[:], offs)
-        for t in range(PACK):
+        for t in range(SLOTS):
             nc.sync.dma_start(out=x_planes[t][:], in_=x_rows[t])
         for (a, b), tile in zip(res_spans, res_sb):
             nc.sync.dma_start(out=tile[:], in_=res_rows[:, :, a:b])
 
-        turned = psum.tile([P, PACK, P], F32, name="bank", tag="bank")
-        for c in range(PACK):
+        turned = psum.tile([P, HALF // P, P], F32, name="bank", tag="bank")
+        for c in range(HALF // P):
             nc.tensor.transpose(turned[:, c, :], head_rows[:, c * P : (c + 1) * P], ident[:])
         for s, weights in enumerate((z_wgt, x_wgt)):
             for e in range(2):
-                spread = ring.tile([P, PACK, HEADS, 16], F32, name="spread", tag="spread")
-                first = 16 * s + e
-                nc.scalar.copy(
-                    out=spread[:],
-                    in_=turned[:, :, first : first + 15 : 2].unsqueeze(3).to_broadcast([P, PACK, HEADS, 16]),
-                )
-                back = psum.tile([P, PACK, P], F32, name="bank", tag="bank")
-                for c in range(PACK):
+                spread = ring.tile([P, HALF // P, HEADS, GROUP], F32, name="spread", tag="spread")
+                first = 2 * HEADS * s + e
+                heads = turned[:, :, first : first + 2 * HEADS - 1 : 2]
+                nc.scalar.copy(out=spread[:], in_=heads.unsqueeze(3).to_broadcast([P, HALF // P, HEADS, GROUP]))
+                back = psum.tile([P, HALF // P, P], F32, name="bank", tag="bank")
+                for c in range(HALF // P):
                     nc.tensor.transpose(back[:, c, :], spread[:, c].rearrange("p g r -> p (g r)"), ident[:])
                 nc.scalar.copy(out=weights[:, e * HALF : (e + 1) * HALF], in_=back[:].rearrange("p c j -> p (c j)"))
 
         nc.vector.tensor_copy(
-            out=wa_codes[:].rearrange("p (t m b) -> p m t b", t=PACK, b=2),
-            in_=wa_raw[:].rearrange("p (m t b) -> p m t b", t=PACK, b=2),
+            out=wa_codes[:].rearrange("p (t m b) -> p t m b", t=SLOTS, b=2),
+            in_=wa_raw[:].rearrange("p (m t b) -> p t m b", t=SLOTS, b=2),
         )
         nc.vector.tensor_copy(
-            out=wa_sc[:].rearrange("p (t m) -> p m t", t=PACK), in_=wa_sraw[:].rearrange("p (m t) -> p m t", t=PACK)
+            out=wa_sc[:].rearrange("p (t m) -> p t m", t=SLOTS), in_=wa_sraw[:].rearrange("p (m t) -> p t m", t=SLOTS)
         )
         nc.vector.tensor_copy(
-            out=wb_bf[:].rearrange("p (t m i) -> p m i t", t=PACK, i=PACK),
-            in_=wb_raw[:].rearrange("p i (m t) -> p m i t", t=PACK),
+            out=wb_bf[:].rearrange("p (u e m i) -> p u m i e", u=2, e=2, i=SLOTS),
+            in_=wb_raw[:].rearrange("p i (m u e) -> p u m i e", u=2, e=2),
         )
         nc.vector.quantize_mx(out=wb_codes[:].bitcast(E4M3), scales=wb_sc[:], in_=wb_bf[:])
 
-        def gather(dst, planes, lst, weights, t, c0, c1):
-            nc.vector.tensor_tensor(
-                dst[:, t, c0:c1], planes[t][:].indirect(lst[:, c0 // 16 : c1 // 16]), weights[:, c0:c1], MULT
-            )
+        def gather(dst, planes, places, weights, t, c0, c1):
+            window = planes[t][:].indirect(places[:, c0 // GROUP : c1 // GROUP])
+            nc.vector.tensor_tensor(dst[:, t, c0:c1], window, weights[:, c0:c1], MULT)
 
-        def quantise(codes, scales, bf, c0, c1):
-            nc.vector.quantize_mx(
-                out=codes[:, c0:c1].bitcast(E4M3), scales=scales[:, c0:c1], in_=bf[:].rearrange("p j t -> p (j t)")
-            )
-
-        def rounded(src, tag, copy=nc.scalar.copy):
-            bf = ring.tile([P, src.shape[2], PACK], BF16, name=tag, tag=tag, align_bytes=64, bufs=4)
-            interleave(copy, bf[:], src)
+        def round_into(bf, src):
+            nc.scalar.copy(out=bf.rearrange("p (c i) t -> p c t i", i=4), in_=src.rearrange("p t (c i) -> p c t i", i=4))
             return bf
 
-        def products(w_codes, w_sc, codes, scales, c0, c1):
-            per_bank = min(PACK, BANK // (c1 - c0))
+        def rounded(src, tag):
+            bf = ring.tile([P, src.shape[2], SLOTS], BF16, name=tag, tag=tag, align_bytes=64, bufs=4)
+            return round_into(bf[:], src)
+
+        def quantise(codes, scales, bf, c):
+            c0, c1 = chunks[c]
+            nc.vector.quantize_mx(
+                out=codes[:, c0:c1].bitcast(E4M3), scales=scales[:, c0:c1], in_=bf.rearrange("p j t -> p (j t)")
+            )
+
+        def wb_cols(t):
+            return wb_codes[:, t * P : (t + 1) * P].bitcast(E4M3)
+
+        def wa_cols(t):
+            return wa_codes[:, 2 * t * P : 2 * (t + 1) * P].bitcast(E2M1)
+
+        def products(c, w_cols, w_sc, codes, scales):
+            c0, c1 = chunks[c]
+            per_bank = BANK // (c1 - c0)
             banks = []
-            for t0 in range(0, PACK, per_bank):
+            for t0 in range(0, SLOTS, per_bank):
                 bank = psum.tile([P, per_bank, c1 - c0], F32, name="bank", tag="bank")
                 for u in range(per_bank):
                     t = t0 + u
                     nc.tensor.matmul_mx(
                         out=bank[:, u, :],
-                        lhsT=w_codes(t),
+                        lhsT=w_cols(t),
                         lhsT_scale=w_sc[:, t * P : (t + 1) * P],
                         rhs=codes[:, c0:c1].bitcast(E4M3),
                         rhs_scale=scales[:, c0:c1],
@@ -176,77 +182,68 @@ def tile_list_gate_resP_kernel(
                 banks.append((slice(t0, t0 + per_bank), bank))
             return banks
 
-        def wb_cols(t):
-            return wb_codes[:, t * P : (t + 1) * P].bitcast(E4M3)
-
-        def wa_cols(t):
-            return wa_codes[:, 2 * t * P : 2 * (t + 1) * P].bitcast(E2M1)
-
         for e in range(2):
             gather(zg, z_planes, z_list, z_wgt, 0, e * HALF, (e + 1) * HALF)
-        for t in range(1, PACK - 1):
+        for t in range(1, SLOTS - 1):
             gather(zg, z_planes, z_list, z_wgt, t, 0, J)
-        for c0, c1 in spans:
-            gather(zg, z_planes, z_list, z_wgt, PACK - 1, c0, c1)
+        for c0, c1 in spans_of(Z_GATHER_CUTS):
+            gather(zg, z_planes, z_list, z_wgt, SLOTS - 1, c0, c1)
         gather(xg, x_planes, x_list, x_wgt, 0, 0, J)
 
-
-        def gated(c):
-            c0, c1 = spans[c]
-            for rows, bank in products(wb_cols, wb_sc, z_codes, z_sc, c0, c1):
-                nc.scalar.activation(out=gate[c][:, rows, :], in_=bank[:], func=SIGMOID)
-
-        def front(c):
-            c0, c1 = spans[c]
-            quantise(x_codes, x_sc, rounded(xg[:, :, c0:c1], "x_bf"), c0, c1)
-            return products(wa_cols, wa_sc, x_codes, x_sc, c0, c1)
-
-        def combined(c, banks):
-            c0, c1 = spans[c]
-            h = [a <= c0 < b for a, b in res_spans].index(True)
-            a = res_spans[h][0]
-            prod = ring.tile([P, PACK, c1 - c0], F32, name="prod", tag="prod", bufs=1)
-            o = ring.tile([P, PACK, c1 - c0], F32, name="o", tag="o", bufs=3)
-            pairs = (slice(0, 2), slice(2, 4))
-            for k, rows in enumerate(pairs):
-                ya = banks[k][1][:] if len(banks) == 2 else banks[0][1][:, rows, :]
-                nc.vector.tensor_tensor(prod[:, rows, :], ya, gate[c][:, rows, :], MULT)
-            for rows in pairs:
-                nc.vector.tensor_tensor(o[:, rows, :], prod[:, rows, :], res_sb[h][:, rows, c0 - a : c1 - a], ADD)
-            nc.sync.dma_start(out=out_rows[:, :, c0:c1], in_=o[:])
-            return rounded(o[:], "o_bf")
-
-        def planes(c, bf):
-            c0, c1 = spans[c]
-            quantise(o_codes, o_sc, bf, c0, c1)
-            if c1 in WORD_CUTS:
-                a = WORD_CUTS[WORD_CUTS.index(c1) - 1]
-                nc.sync.dma_start(out=out_words[:, a:c1], in_=o_codes[:, a:c1].bitcast(I32))
-
-        for c, (c0, c1) in enumerate(spans):
-            quantise(z_codes, z_sc, rounded(zg[:, :, c0:c1], "z_bf"), c0, c1)
-        for c in range(chunks):
-            gated(c)
-        for t in (1, 2):
+        for c, (c0, c1) in enumerate(chunks):
+            quantise(z_codes, z_sc, rounded(zg[:, :, c0:c1], "z_bf"), c)
+        for c in range(len(chunks)):
+            for slots, bank in products(c, wb_cols, wb_sc, z_codes, z_sc):
+                nc.scalar.activation(out=gate[c][:, slots, :], in_=bank[:], func=SIGMOID)
+        for t in range(1, SLOTS - 1):
             gather(xg, x_planes, x_list, x_wgt, t, 0, J)
-        for c0, c1 in spans[:3]:
-            gather(xg, x_planes, x_list, x_wgt, PACK - 1, c0, c1)
-        lent = xg[:, PACK - 1, spans[3][0] : spans[3][1]].bitcast(BF16).rearrange("p (j t) -> p j t", t=PACK)
-        interleave(nc.scalar.copy, lent, xg[:, :, spans[0][0] : spans[0][1]])
-        quantise(x_codes, x_sc, lent, *spans[0])
-        banks = {0: products(wa_cols, wa_sc, x_codes, x_sc, *spans[0])}
-        for c0, c1 in spans[3:]:
-            gather(xg, x_planes, x_list, x_wgt, PACK - 1, c0, c1)
-        banks[1] = front(1)
-        done = {}
-        for c in range(chunks):
-            if c + 2 < chunks:
-                banks[c + 2] = front(c + 2)
-            if c >= 2:
-                planes(c - 2, done[c - 2])
-            done[c] = combined(c, banks[c])
-        for c in range(chunks - 2, chunks):
-            planes(c, done[c])
+
+        last_piece = spans_of(X_GATHER_CUTS)[-1]
+        for c0, c1 in spans_of(X_GATHER_CUTS)[:-1]:
+            gather(xg, x_planes, x_list, x_wgt, SLOTS - 1, c0, c1)
+        first_width = CHUNK_CUTS[1]
+        lent = xg[:, SLOTS - 1, last_piece[0] : last_piece[0] + 2 * first_width].bitcast(BF16)
+        first_bf = round_into(lent.rearrange("p (j t) -> p j t", t=SLOTS), xg[:, :, 0:first_width])
+        quantise(x_codes, x_sc, first_bf, 0)
+        ya_banks = [products(0, wa_cols, wa_sc, x_codes, x_sc)]
+        gather(xg, x_planes, x_list, x_wgt, SLOTS - 1, *last_piece)
+
+        def combined(c):
+            c0, c1 = chunks[c]
+            banks = ya_banks[c]
+            h = [a <= c0 < b for a, b in res_spans].index(True)
+            given = res_sb[h][:, :, c0 - RES_CUTS[h] : c1 - RES_CUTS[h]]
+            o = keep.tile([P, SLOTS, c1 - c0], F32, name=f"o{c}")
+            prod = ring.tile([P, SLOTS, c1 - c0], F32, name="prod", tag="prod", bufs=1)
+            pairs = (slice(0, 2), slice(2, 4))
+            for k, slots in enumerate(pairs):
+                ya = banks[k][1][:] if len(banks) == 2 else banks[0][1][:, slots, :]
+                nc.vector.tensor_tensor(prod[:, slots, :], ya, gate[c][:, slots, :], MULT)
+            for slots in pairs:
+                nc.vector.tensor_tensor(o[:, slots, :], prod[:, slots, :], given[:, slots, :], ADD)
+            bf = rounded(o[:], "o_bf")
+            nc.sync.dma_start(out=out_rows[:, :, c0:c1], in_=o[:])
+            return bf
+
+        def packed(c, bf):
+            quantise(o_codes, o_sc, bf, c)
+            end = chunks[c][1]
+            if end in WORD_CUTS:
+                start = WORD_CUTS[WORD_CUTS.index(end) - 1]
+                nc.sync.dma_start(out=out_words[:, start:end], in_=o_codes[:, start:end].bitcast(I32))
+
+        o_bf = []
+        for c, (c0, c1) in enumerate(chunks):
+            while len(ya_banks) < len(chunks) and chunks[len(ya_banks)][0] < c1 + AHEAD:
+                ahead = len(ya_banks)
+                quantise(x_codes, x_sc, rounded(xg[:, :, slice(*chunks[ahead])], "x_bf"), ahead)
+                ya_banks.append(products(ahead, wa_cols, wa_sc, x_codes, x_sc))
+            if c >= BEHIND:
+                packed(c - BEHIND, o_bf[c - BEHIND])
+            o_bf.append(combined(c))
+        for c in range(len(chunks) - BEHIND, len(chunks)):
+            packed(c, o_bf[c])
+
         for q in range(4):
             queue = nc.sync if q % 2 == 0 else nc.scalar
             queue.dma_start(

from contextlib import ExitStack

import concourse.mybir as mybir
from concourse.masks import make_identity

K, N, T, J = 512, 512, 2048, 1024
FLOPS = 2 * 2 * K * N * J

F32 = mybir.dt.float32
BF16 = mybir.dt.bfloat16
I32 = mybir.dt.int32
U32 = mybir.dt.uint32
U16 = mybir.dt.uint16
U8 = mybir.dt.uint8
E4M3 = mybir.dt.float8_e4m3fn_x4
E2M1 = mybir.dt.float4_e2m1fn_x4
MULT = mybir.AluOpType.mult
ADD = mybir.AluOpType.add
SIGMOID = mybir.ActivationFunctionType.Sigmoid

P = 128
SLOTS = 4
BANK = 512
HEADS = 8
GROUP = 16
HALF = J // 2

CHUNK_CUTS = [0, 128, 384, 640, 896, 1024]
Z_GATHER_CUTS = [0, 384, 1024]
X_GATHER_CUTS = [0, 128, 640, 1024]
RES_CUTS = [0, 384, 1024]
WORD_CUTS = [0, 384, 896, 1024]
AHEAD = 256
BEHIND = 2


def spans_of(cuts):
    return list(zip(cuts[:-1], cuts[1:]))


def tile_list_gate_resP_kernel(
    tc, xT, wgt, zT, wgt2, wa_words, wa_scales, wb, res, offs, offs2, out_0, out_1, out_2
):
    nc = tc.nc
    chunks = spans_of(CHUNK_CUTS)
    res_spans = spans_of(RES_CUTS)

    with ExitStack() as ctx:
        keep = ctx.enter_context(tc.tile_pool(name="keep", bufs=1))
        ring = ctx.enter_context(tc.tile_pool(name="ring", bufs=2))
        psum = ctx.enter_context(tc.psum_pool(name="psum", bufs=8))

        x_list = keep.tile([P, J // GROUP], U16, name="x_list")
        z_list = keep.tile([P, J // GROUP], U16, name="z_list")
        x_planes = [keep.tile([P, T], F32, name=f"x_plane{t}") for t in range(SLOTS)]
        z_planes = [keep.tile([P, T], F32, name=f"z_plane{t}") for t in range(SLOTS)]
        ident = keep.tile([P, P], F32, name="ident")
        head_rows = keep.tile([P, HALF], F32, name="head_rows")
        x_wgt = keep.tile([P, J], F32, name="x_wgt")
        z_wgt = keep.tile([P, J], F32, name="z_wgt")
        wa_raw = keep.tile([P, 2 * N], U8, name="wa_raw", align_bytes=64)
        wa_sraw = keep.tile([P, N], U8, name="wa_sraw", align_bytes=64)
        wa_codes = keep.tile([P, 2 * N], U8, name="wa_codes", align_bytes=64)
        wa_sc = keep.tile([P, N], U8, name="wa_sc", align_bytes=64)
        wb_raw = keep.tile([P, SLOTS, N], F32, name="wb_raw")
        wb_bf = keep.tile([P, SLOTS * N], BF16, name="wb_bf", align_bytes=64)
        wb_codes = keep.tile([P, N], U32, name="wb_codes", align_bytes=64)
        wb_sc = keep.tile([P, N], U8, name="wb_sc", align_bytes=64)
        res_sb = [keep.tile([P, SLOTS, b - a], F32, name=f"res{a}") for a, b in res_spans]
        xg_flat = keep.tile([P, SLOTS * J], F32, name="xg", align_bytes=64)
        xg = xg_flat[:].rearrange("p (t j) -> p t j", t=SLOTS)
        zg = keep.tile([P, SLOTS, J], F32, name="zg")
        x_codes = keep.tile([P, J], U32, name="x_codes", align_bytes=64)
        x_sc = keep.tile([P, J], U8, name="x_sc", align_bytes=64)
        z_codes = keep.tile([P, J], U32, name="z_codes", align_bytes=64)
        z_sc = keep.tile([P, J], U8, name="z_sc", align_bytes=64)
        gate = [keep.tile([P, SLOTS, b - a], F32, name=f"gate{a}") for a, b in chunks]
        o_codes = keep.tile([P, J], U32, name="o_codes", align_bytes=64)
        o_sc = keep.tile([P, J], U8, name="o_sc", align_bytes=64)

        x_rows = xT.rearrange("(p t) j -> t p j", t=SLOTS)
        z_rows = zT.rearrange("(p t) j -> t p j", t=SLOTS)
        res_rows = res.rearrange("(p t) j -> p t j", t=SLOTS)
        out_rows = out_0.rearrange("(p t) j -> p t j", t=SLOTS)
        out_words = out_1[0].rearrange("p j i -> p (j i)").bitcast(I32)

        def half_rows(w):
            step = 7 * J + HALF
            flat = w.rearrange("p j -> (p j)")[7 * J : 7 * J + 2 * HEADS * step]
            return flat.rearrange("(q s) -> q s", s=step)[:, :HALF]

        nc.gpsimd.memset(wa_sraw[:].bitcast(I32), 0)
        nc.vector.memset(head_rows[32:64, :], 0.0)
        nc.vector.memset(head_rows[64:128, :], 0.0)
        make_identity(nc, ident[:])

        nc.sync.dma_start(out=head_rows[0:16, :], in_=half_rows(wgt2))
        nc.sync.dma_start(out=head_rows[16:32, :], in_=half_rows(wgt))
        for q in range(4):
            nc.scalar.dma_start(
                out=wa_sraw[32 * q : 32 * q + 4, :].bitcast(I32), in_=wa_scales[0, 4 * q : 4 * q + 4, :].bitcast(I32)
            )
        nc.sync.dma_start(out=wa_raw[:].bitcast(I32), in_=wa_words[0].bitcast(I32))
        nc.sync.dma_start(out=wb_raw[:], in_=wb.rearrange("(p t) n -> p t n", t=SLOTS))
        nc.sync.dma_start(z_list[:], offs2)
        for t in range(SLOTS):
            nc.sync.dma_start(out=z_planes[t][:], in_=z_rows[t])
        nc.sync.dma_start(x_list[:], offs)
        for t in range(SLOTS):
            nc.sync.dma_start(out=x_planes[t][:], in_=x_rows[t])
        for (a, b), tile in zip(res_spans, res_sb):
            nc.sync.dma_start(out=tile[:], in_=res_rows[:, :, a:b])

        turned = psum.tile([P, HALF // P, P], F32, name="bank", tag="bank")
        for c in range(HALF // P):
            nc.tensor.transpose(turned[:, c, :], head_rows[:, c * P : (c + 1) * P], ident[:])
        for s, weights in enumerate((z_wgt, x_wgt)):
            for e in range(2):
                spread = ring.tile([P, HALF // P, HEADS, GROUP], F32, name="spread", tag="spread")
                first = 2 * HEADS * s + e
                heads = turned[:, :, first : first + 2 * HEADS - 1 : 2]
                nc.scalar.copy(out=spread[:], in_=heads.unsqueeze(3).to_broadcast([P, HALF // P, HEADS, GROUP]))
                back = psum.tile([P, HALF // P, P], F32, name="bank", tag="bank")
                for c in range(HALF // P):
                    nc.tensor.transpose(back[:, c, :], spread[:, c].rearrange("p g r -> p (g r)"), ident[:])
                nc.scalar.copy(out=weights[:, e * HALF : (e + 1) * HALF], in_=back[:].rearrange("p c j -> p (c j)"))

        nc.vector.tensor_copy(
            out=wa_codes[:].rearrange("p (t m b) -> p t m b", t=SLOTS, b=2),
            in_=wa_raw[:].rearrange("p (m t b) -> p t m b", t=SLOTS, b=2),
        )
        nc.vector.tensor_copy(
            out=wa_sc[:].rearrange("p (t m) -> p t m", t=SLOTS), in_=wa_sraw[:].rearrange("p (m t) -> p t m", t=SLOTS)
        )
        nc.vector.tensor_copy(
            out=wb_bf[:].rearrange("p (u e m i) -> p u m i e", u=2, e=2, i=SLOTS),
            in_=wb_raw[:].rearrange("p i (m u e) -> p u m i e", u=2, e=2),
        )
        nc.vector.quantize_mx(out=wb_codes[:].bitcast(E4M3), scales=wb_sc[:], in_=wb_bf[:])

        def gather(dst, planes, places, weights, t, c0, c1):
            window = planes[t][:].indirect(places[:, c0 // GROUP : c1 // GROUP])
            nc.vector.tensor_tensor(dst[:, t, c0:c1], window, weights[:, c0:c1], MULT)

        def round_into(bf, src):
            nc.scalar.copy(out=bf.rearrange("p (c i) t -> p c t i", i=4), in_=src.rearrange("p t (c i) -> p c t i", i=4))
            return bf

        def rounded(src, tag):
            bf = ring.tile([P, src.shape[2], SLOTS], BF16, name=tag, tag=tag, align_bytes=64, bufs=4)
            return round_into(bf[:], src)

        def quantise(codes, scales, bf, c):
            c0, c1 = chunks[c]
            nc.vector.quantize_mx(
                out=codes[:, c0:c1].bitcast(E4M3), scales=scales[:, c0:c1], in_=bf.rearrange("p j t -> p (j t)")
            )

        def wb_cols(t):
            return wb_codes[:, t * P : (t + 1) * P].bitcast(E4M3)

        def wa_cols(t):
            return wa_codes[:, 2 * t * P : 2 * (t + 1) * P].bitcast(E2M1)

        def products(c, w_cols, w_sc, codes, scales):
            c0, c1 = chunks[c]
            per_bank = BANK // (c1 - c0)
            banks = []
            for t0 in range(0, SLOTS, per_bank):
                bank = psum.tile([P, per_bank, c1 - c0], F32, name="bank", tag="bank")
                for u in range(per_bank):
                    t = t0 + u
                    nc.tensor.matmul_mx(
                        out=bank[:, u, :],
                        lhsT=w_cols(t),
                        lhsT_scale=w_sc[:, t * P : (t + 1) * P],
                        rhs=codes[:, c0:c1].bitcast(E4M3),
                        rhs_scale=scales[:, c0:c1],
                        start=True,
                        stop=True,
                    )
                banks.append((slice(t0, t0 + per_bank), bank))
            return banks

        for e in range(2):
            gather(zg, z_planes, z_list, z_wgt, 0, e * HALF, (e + 1) * HALF)
        for t in range(1, SLOTS - 1):
            gather(zg, z_planes, z_list, z_wgt, t, 0, J)
        for c0, c1 in spans_of(Z_GATHER_CUTS):
            gather(zg, z_planes, z_list, z_wgt, SLOTS - 1, c0, c1)
        gather(xg, x_planes, x_list, x_wgt, 0, 0, J)

        for c, (c0, c1) in enumerate(chunks):
            quantise(z_codes, z_sc, rounded(zg[:, :, c0:c1], "z_bf"), c)
        for c in range(len(chunks)):
            for slots, bank in products(c, wb_cols, wb_sc, z_codes, z_sc):
                nc.scalar.activation(out=gate[c][:, slots, :], in_=bank[:], func=SIGMOID)
        for t in range(1, SLOTS - 1):
            gather(xg, x_planes, x_list, x_wgt, t, 0, J)

        last_piece = spans_of(X_GATHER_CUTS)[-1]
        for c0, c1 in spans_of(X_GATHER_CUTS)[:-1]:
            gather(xg, x_planes, x_list, x_wgt, SLOTS - 1, c0, c1)
        first_width = CHUNK_CUTS[1]
        lent = xg[:, SLOTS - 1, last_piece[0] : last_piece[0] + 2 * first_width].bitcast(BF16)
        first_bf = round_into(lent.rearrange("p (j t) -> p j t", t=SLOTS), xg[:, :, 0:first_width])
        quantise(x_codes, x_sc, first_bf, 0)
        ya_banks = [products(0, wa_cols, wa_sc, x_codes, x_sc)]
        gather(xg, x_planes, x_list, x_wgt, SLOTS - 1, *last_piece)

        def combined(c):
            c0, c1 = chunks[c]
            banks = ya_banks[c]
            h = [a <= c0 < b for a, b in res_spans].index(True)
            given = res_sb[h][:, :, c0 - RES_CUTS[h] : c1 - RES_CUTS[h]]
            o = keep.tile([P, SLOTS, c1 - c0], F32, name=f"o{c}")
            prod = ring.tile([P, SLOTS, c1 - c0], F32, name="prod", tag="prod", bufs=1)
            pairs = (slice(0, 2), slice(2, 4))
            for k, slots in enumerate(pairs):
                ya = banks[k][1][:] if len(banks) == 2 else banks[0][1][:, slots, :]
                nc.vector.tensor_tensor(prod[:, slots, :], ya, gate[c][:, slots, :], MULT)
            for slots in pairs:
                nc.vector.tensor_tensor(o[:, slots, :], prod[:, slots, :], given[:, slots, :], ADD)
            bf = rounded(o[:], "o_bf")
            nc.sync.dma_start(out=out_rows[:, :, c0:c1], in_=o[:])
            return bf

        def packed(c, bf):
            quantise(o_codes, o_sc, bf, c)
            end = chunks[c][1]
            if end in WORD_CUTS:
                start = WORD_CUTS[WORD_CUTS.index(end) - 1]
                nc.sync.dma_start(out=out_words[:, start:end], in_=o_codes[:, start:end].bitcast(I32))

        o_bf = []
        for c, (c0, c1) in enumerate(chunks):
            while len(ya_banks) < len(chunks) and chunks[len(ya_banks)][0] < c1 + AHEAD:
                ahead = len(ya_banks)
                quantise(x_codes, x_sc, rounded(xg[:, :, slice(*chunks[ahead])], "x_bf"), ahead)
                ya_banks.append(products(ahead, wa_cols, wa_sc, x_codes, x_sc))
            if c >= BEHIND:
                packed(c - BEHIND, o_bf[c - BEHIND])
            o_bf.append(combined(c))
        for c in range(len(chunks) - BEHIND, len(chunks)):
            packed(c, o_bf[c])

        for q in range(4):
            queue = nc.sync if q % 2 == 0 else nc.scalar
            queue.dma_start(
                out=out_2[0, 4 * q : 4 * q + 4, :].bitcast(I32), in_=o_sc[32 * q : 32 * q + 4, :].bitcast(I32)
            )
